import numpy as np
import ml_dtypes


def mxq(x, axis, fmt="e4m3"):
    dtype, down = {"e4m3": (ml_dtypes.float8_e4m3fn, 7), "e5m2": (ml_dtypes.float8_e5m2, 14)}[fmt]
    v = np.moveaxis(np.asarray(x, np.float32).astype(ml_dtypes.bfloat16).astype(np.float64), axis, -1)
    blocks = v.reshape(v.shape[:-1] + (-1, 32))
    amax = np.abs(blocks).max(-1, keepdims=True)
    byte = np.maximum(np.where(amax > 0, np.frexp(amax)[1] - 1 + 127, 0) - down, 1)
    scale = np.exp2(byte - 127.0)
    codes = (blocks / scale).astype(np.float32).astype(dtype).astype(np.float64)
    return np.moveaxis((codes * scale).reshape(v.shape), -1, axis)


WIDE = False


def mx_kscale(k):
    if not WIDE:
        return np.ones(k)
    levels = np.array([10, -10, 5, -5, 0])
    if k % 512:
        return np.exp2(np.random.permutation(np.resize(levels, k // 32))).repeat(32)
    a = np.empty((k // 512, 16))
    for p in range(k // 512):
        a[p, :8] = np.random.permutation(np.resize(levels, 8))
        for g in range(8):
            far = levels[np.abs(levels - a[p, g]) >= 10]
            a[p, g + 8] = far[np.random.randint(len(far))]
    return np.exp2(a.ravel()).repeat(32)


def f64(x):
    return np.asarray(x).astype(np.float64)


def striped(idx):
    return np.tile(idx.reshape(-1, 16).T, (8, 1)).astype(np.uint16)


def unstriped(offs):
    return offs[:16].T.reshape(-1).astype(np.int64)


E2M1 = np.array([0.0, 0.5, 1.0, 1.5, 2.0, 3.0, 4.0, 6.0, -0.0, -0.5, -1.0, -1.5, -2.0, -3.0, -4.0, -6.0])


def pack_fp4(w):
    k, n = w.shape
    w = f64(np.asarray(w, np.float32).astype(ml_dtypes.bfloat16)).reshape(k // 32, 32, n)
    amax = np.abs(w).max(1)
    mant, ex = np.frexp(amax / 6.0)
    byte = np.clip(np.where(amax > 0, np.where(mant > 0.5, ex, ex - 1) + 127, 1), 1, 254)
    scaled = (w * np.exp2(127.0 - byte)[:, None, :]).reshape(k, n).astype(np.float32)
    c = np.ascontiguousarray(scaled.reshape(k // 512, 128, 4, n).transpose(0, 1, 3, 2)).astype(ml_dtypes.float4_e2m1fn).view(np.uint8) & 0xF
    words = (c[..., 0::2] | (c[..., 1::2] << 4)).reshape(k // 512, 128, 2 * n)
    return np.ascontiguousarray(words), np.ascontiguousarray(byte.astype(np.uint8).reshape(k // 512, 16, n))


def unpack_fp4(words, scales):
    g, _, n = scales.shape
    words = np.ascontiguousarray(words).reshape(g, 128, n, 2)
    nib = np.empty((g, 128, n, 4), np.uint8)
    nib[..., 0::2] = words & 0xF
    nib[..., 1::2] = words >> 4
    vals = E2M1[nib] * np.repeat(np.exp2(scales.astype(np.float64) - 127.0), 8, axis=1)[..., None]
    return vals.transpose(0, 1, 3, 2).reshape(g * 512, n)


def silu(v):
    return v / (1.0 + np.exp(-np.maximum(v, -700.0)))

def planes(y):
    n, m = y.shape
    v = y.astype(np.float32).astype(ml_dtypes.bfloat16).astype(np.float64).reshape(n // 32, 32, m)
    top = np.abs(v).max(1)
    byte = np.clip(np.where(top > 0, np.frexp(top)[1] - 1 + 127 - 7, 1), 1, 254)
    codes = (v * np.exp2(127.0 - byte)[:, None, :]).reshape(n, m).astype(np.float32).astype(ml_dtypes.float8_e4m3fn).view(np.uint8)
    words = codes.reshape(n // 512, 128, 4, m).transpose(0, 1, 3, 2)
    return np.ascontiguousarray(words), np.ascontiguousarray(byte.astype(np.uint8).reshape(n // 512, 16, m))


K, T, H, J, U = 1024, 512, 512, 512, 1024


def setup_inputs():
    n = np.random.standard_normal
    s = mx_kscale(K)[:, None]
    u = mx_kscale(H)
    r = mx_kscale(J)[:, None]
    packed_xT = pack_fp4(n((K, T)) * s)
    return {
        "x_words": packed_xT[0],
        "x_scales": packed_xT[1],
        "aT": (n((J, U)) * r).astype(np.float32),
        "w1": (n((K, H)) / np.sqrt(K) / s * u).astype(np.float32),
        "w3": (n((J, H)) / np.sqrt(J) / r).astype(np.float32),
        "w2": (n((H, H)) / np.sqrt(2 * H) / u[:, None]).astype(np.float32),
        "pos1": striped(np.random.permutation(T)),
        "pos2": striped(np.random.permutation(T)),
    }


def reference(x_words, x_scales, aT, w1, w3, w2, pos1, pos2):
    xq = unpack_fp4(x_words, x_scales)
    h = silu(mxq(f64(w1), 0, "e4m3").T @ xq)
    f = mxq(f64(w3), 0, "e4m3").T @ mxq(f64(aT), 0, "e4m3")
    z = h[:, unstriped(pos1)] * f[:, :T] + h[:, unstriped(pos2)] * f[:, T:2 * T]
    out_0 = silu(mxq(f64(w2), 0, "e4m3").T @ mxq(z, 0, "e4m3"))
    return (out_0,) + planes(out_0)

@@ -1,0 +1,247 @@
+from contextlib import ExitStack
+
+import concourse.mybir as mybir
+
+K, T, H, J = 1024, 512, 512, 512
+FLOPS = 2 * (K * H * T + J * H * 2 * T + H * H * T)
+
+F32 = mybir.dt.float32
+BF16 = mybir.dt.bfloat16
+I32 = mybir.dt.int32
+U32 = mybir.dt.uint32
+U16 = mybir.dt.uint16
+U8 = mybir.dt.uint8
+FP8X4 = mybir.dt.float8_e4m3fn_x4
+FP4X4 = mybir.dt.float4_e2m1fn_x4
+SILU = mybir.ActivationFunctionType.Silu
+MULT = mybir.AluOpType.mult
+ADD = mybir.AluOpType.add
+
+P = 128
+
+
+def tile_picked_wdime_silu_lo_kernel(
+    tc, x_words, x_scales, aT, w1, w3, w2, pos1, pos2, out_0, out_1, out_2
+):
+    nc = tc.nc
+    with ExitStack() as ctx:
+        sb = ctx.enter_context(tc.tile_pool(name="sb", bufs=1))
+        ps = ctx.enter_context(tc.psum_pool(name="ps", bufs=1))
+
+        def tile(name, shape, dtype):
+            return sb.tile(shape, dtype, name=name, align_bytes=64)[:]
+
+        def bank(b):
+            return ps.tile([P, 512], F32, name="bank%d" % b)[:]
+
+        def copy_on(engine, out, in_):
+            if engine == "v":
+                nc.vector.tensor_copy(out=out, in_=in_)
+            else:
+                nc.scalar.copy(out=out, in_=in_)
+
+        def load(raw, rows):
+            nc.sync.dma_start(out=raw, in_=rows.rearrange("(p j) w -> p j w", j=4))
+            return raw
+
+        def round_weights(dealt, raw, u, engine):
+            src = raw.rearrange("p j (m t) -> p m j t", t=4)[:, :, :, 2 * u : 2 * u + 2]
+            copy_on(engine, dealt.rearrange("p (t m j) -> p m j t", t=2, j=4), src)
+            return dealt
+
+        def round_columns(woven, planes, engine):
+            copy_on(
+                engine,
+                woven.rearrange("p (c i j) -> p c j i", i=4, j=4),
+                planes.rearrange("p j (c i) -> p c j i", i=4),
+            )
+            return woven
+
+        def quantize(name, woven):
+            width = woven.shape[1] // 4
+            codes = tile(name + "_codes", [P, width], U32)
+            scales = tile(name + "_scales", [P, width], U8)
+            nc.vector.quantize_mx(out=codes.bitcast(FP8X4), scales=scales, in_=woven)
+            return codes, scales
+
+        def product(out, weights, t, rhs, rhs_scale, start=True, stop=True):
+            codes, scales = weights[t // 2]
+            cols = slice(P * (t % 2), P * (t % 2 + 1))
+            nc.tensor.matmul_mx(
+                out=out,
+                lhsT=codes[:, cols].bitcast(FP8X4),
+                lhsT_scale=scales[:, cols],
+                rhs=rhs,
+                rhs_scale=rhs_scale,
+                start=start,
+                stop=stop,
+            )
+
+        def bf(name, n):
+            return tile(name, [P, n], BF16)
+
+        def f32(name, a, b):
+            return tile(name, [P, a, b], F32)
+
+        lists = [sb.tile([P, T // 16], U16, name="list0"), sb.tile([P, T // 16], U16, name="list1")]
+        h = [sb.tile([P, T], F32, name="h%d" % t) for t in range(4)]
+        xs = tile("xs", [P, 2, T], U8)
+        xw = tile("xw", [P, 2, 2 * T], U8)
+        words = tile("words", [P, T], U32)
+        out_scales = tile("out_scales", [P, T], U8)
+        y_rows = out_0.rearrange("(p t) v -> p t v", t=4)
+        word_rows = out_1[0].rearrange("p c r -> p (c r)").bitcast(I32)
+
+        warm = tile("warm", [P, 1], F32)
+        warmed = tile("warmed", [P, 1], F32)
+        nc.vector.memset(warm, 0.0)
+        nc.scalar.activation(out=warmed, in_=warm, func=SILU)
+
+        def load_x():
+            nc.sync.dma_start(out=xw.bitcast(I32), in_=x_words.rearrange("z p c -> p z c").bitcast(I32))
+            for q in range(4):
+                nc.sync.dma_start(
+                    out=xs[32 * q : 32 * q + 4, :, :].bitcast(I32),
+                    in_=x_scales[:, 4 * q : 4 * q + 4, :].rearrange("z r c -> r z c").bitcast(I32),
+                )
+
+        def a_cols(d, v0, width):
+            return aT[:, T * d + v0 : T * d + v0 + width]
+
+        def layer1(acc, w1_q, z, ts):
+            for t in ts:
+                product(acc[t], w1_q, t, xw[:, z, :].bitcast(FP4X4), xs[:, z, :], z == 0, z == 1)
+
+        def finish_h(acc, t):
+            nc.scalar.activation(out=h[t][:], in_=acc[t], func=SILU)
+
+        def filters(name, acc, w3_q, a_q, ts, engine):
+            codes, scales = a_q
+            width = codes.shape[1]
+            for s, t in enumerate(ts):
+                product(acc[:, width * s : width * (s + 1)], w3_q, t, codes.bitcast(FP8X4), scales)
+            f = f32(name, len(ts), width)
+            copy_on(engine, f.rearrange("p s c -> p (s c)"), acc[:, 0 : width * len(ts)])
+            return [f[:, s, :] for s in range(len(ts))]
+
+        def gather(d, v0, t, term, f):
+            width = term.shape[2]
+            offsets = lists[d][:, v0 // 16 : (v0 + width) // 16]
+            nc.vector.tensor_tensor(term[:, t, :], h[t][:].indirect(offsets), f, MULT)
+
+        def gathers(d, v0, term, fs, lo=0):
+            for t in range(4):
+                gather(d, v0, t, term, fs[t][:, lo : lo + term.shape[2]])
+            return term
+
+        def sum_terms(z_bf, term0, term1):
+            nc.vector.tensor_tensor(
+                z_bf.rearrange("p (c i t) -> p c t i", i=4, t=4),
+                term0.rearrange("p t (c i) -> p c t i", i=4),
+                term1.rearrange("p t (c i) -> p c t i", i=4),
+                ADD,
+            )
+            return z_bf
+
+        def project(accs, w2_q, z_q):
+            codes, scales = z_q
+            width = codes.shape[1]
+            per_bank = 4 // len(accs)
+            for t in range(4):
+                s = t % per_bank
+                product(accs[t // per_bank][:, width * s : width * (s + 1)], w2_q, t, codes.bitcast(FP8X4), scales)
+
+        def finish_y(accs, v0, width):
+            y = f32("y%d" % v0, 4, width)
+            per_bank = 4 // len(accs)
+            for b, acc in enumerate(accs):
+                nc.scalar.activation(
+                    out=y[:, per_bank * b : per_bank * (b + 1), :].rearrange("p t c -> p (t c)"),
+                    in_=acc[:, 0 : per_bank * width],
+                    func=SILU,
+                )
+            nc.sync.dma_start(out=y_rows[:, :, v0 : v0 + width], in_=y)
+            return y
+
+        def silu_woven(woven, acc):
+            width = woven.shape[1] // 4
+            nc.scalar.activation(
+                out=woven.rearrange("p (c t) -> p c t", t=4),
+                in_=acc[:, 0 : 4 * width].rearrange("p (t c) -> p c t", t=4),
+                func=SILU,
+            )
+            return woven
+
+        def hand_on(v0, woven_y):
+            cols = slice(v0, v0 + woven_y.shape[1] // 4)
+            nc.vector.quantize_mx(out=words[:, cols].bitcast(FP8X4), scales=out_scales[:, cols], in_=woven_y)
+            nc.sync.dma_start(out=word_rows[:, cols], in_=words[:, cols].bitcast(I32))
+
+        def store_scales():
+            for q in range(4):
+                queue = nc.sync if q % 2 else nc.scalar
+                queue.dma_start(
+                    out=out_2[0, 4 * q : 4 * q + 4, :].bitcast(I32),
+                    in_=out_scales[32 * q : 32 * q + 4, :].bitcast(I32),
+                )
+
+        w3_raw = load(f32("w3_raw", 4, 512), w3)
+        a00 = load(f32("a_raw00", 4, 256), a_cols(0, 0, 256))
+        w1_raw = [load(f32("w1_raw0", 4, 512), w1[0:512, :])]
+        load_x()
+        w1_raw.append(load(f32("w1_raw1", 4, 512), w1[512:1024, :]))
+        a10 = load(f32("a_raw10", 4, 256), a_cols(1, 0, 256))
+        nc.sync.dma_start(lists[0][:], pos1)
+        nc.sync.dma_start(lists[1][:], pos2)
+        a01 = load(f32("a_raw01", 4, 256), a_cols(0, 256, 256))
+        shared = f32("shared", 7, 256)
+        a11 = load(shared[:, 3:7, :], a_cols(1, 256, 256))
+        w2_raw = load(f32("w2_raw", 4, 512), w2)
+
+        woven = [round_weights(bf("w3_bf%d" % u, 1024), w3_raw, u, "vs"[u]) for u in range(2)]
+        w3_q = [quantize("w3_%d" % u, woven[u]) for u in range(2)]
+        q00 = quantize("a00", round_columns(bf("a_bf00", 1024), a00, "v"))
+        f00 = filters("f00a", bank(4), w3_q, q00, [0, 1], "s")
+        f00 = f00 + filters("f00b", bank(5), w3_q, q00, [2, 3], "s")
+        acc_h = [bank(t) for t in range(4)]
+        for z in range(2):
+            woven = [round_weights(bf("w1_bf%d%d" % (z, u), 1024), w1_raw[z], u, "vs"[u]) for u in range(2)]
+            w1_q = [quantize("w1_%d%d" % (z, u), woven[u]) for u in range(2)]
+            layer1(acc_h, w1_q, z, range(4))
+        for t in range(4):
+            finish_h(acc_h, t)
+        q10 = quantize("a10", round_columns(bf("a_bf10", 1024), a10, "v"))
+        f10 = filters("f10a", bank(6), w3_q, q10, [0, 1], "s")
+        f10 = f10 + filters("f10b", bank(7), w3_q, q10, [2, 3], "s")
+        t00 = gathers(0, 0, f32("term00", 4, 256), f00)
+        q01 = quantize("a01", round_columns(bf("a_bf01", 1024), a01, "v"))
+        woven_a = round_columns(bf("a_bf11", 1024), a11, "s")
+        f01 = filters("f01a", bank(4), w3_q, q01, [0, 1], "s")
+        f01 = f01 + filters("f01b", bank(5), w3_q, q01, [2, 3], "s")
+        q11 = quantize("a11", woven_a)
+        woven = [round_weights(bf("w2_bf0", 1024), w2_raw, 0, "s")]
+        f11 = filters("f11a", bank(6), w3_q, q11, [0, 1], "s")
+        f11 = f11 + filters("f11b", bank(7), w3_q, q11, [2, 3], "s")
+        woven.append(round_weights(bf("w2_bf1", 1024), w2_raw, 1, "s"))
+        w2_q = [quantize("w2_%d" % u, woven[u]) for u in range(2)]
+        t10 = gathers(1, 0, shared[:, 0:4, :], f10)
+        z0 = quantize("z0", sum_terms(bf("z_bf0", 1024), t00, t10))
+        acc0 = [bank(0), bank(1)]
+        project(acc0, w2_q, z0)
+        y0 = finish_y(acc0, 0, 256)
+        t01 = gathers(0, 256, f32("term01", 4, 256), f01)
+        t11 = gathers(1, 256, w2_raw[:, :, 0:128], f11)
+        z1 = quantize("z1", sum_terms(bf("z_bf1", 512), t01[:, :, 0:128], t11))
+        acc1 = [bank(2)]
+        project(acc1, w2_q, z1)
+        y1 = finish_y(acc1, 256, 128)
+        t12 = gathers(1, 384, w2_raw[:, :, 128:256], f11, 128)
+        z2 = quantize("z2", sum_terms(bf("z_bf2", 512), t01[:, :, 128:256], t12))
+        acc2 = [bank(3)]
+        project(acc2, w2_q, z2)
+        woven_y2 = silu_woven(bf("y_bf2", 512), acc2[0])
+        finish_y(acc2, 384, 128)
+        hand_on(0, round_columns(bf("y_bf0", 1024), y0, "s"))
+        hand_on(256, round_columns(bf("y_bf1", 512), y1, "s"))
+        hand_on(384, woven_y2)
+        store_scales()

@@ -49,6 +49,11 @@ def tile_picked_wdime_silu_lo_kernel(
             copy_on(engine, dealt.rearrange("p (t m j) -> p m j t", t=2, j=4), src)
             return dealt
 
+        def round_half(dealt, raw, u, half, engine):
+            src = raw.rearrange("p j (m t) -> p m j t", t=4)[:, :, :, 2 * u : 2 * u + 2]
+            dst = dealt.rearrange("p (t m j) -> p m j t", t=2, j=4)[:, 64 * half : 64 * (half + 1), :, :]
+            copy_on(engine, dst, src)
+
         def round_columns(woven, planes, engine):
             copy_on(
                 engine,
@@ -65,8 +70,9 @@ def tile_picked_wdime_silu_lo_kernel(
             return codes, scales
 
         def product(out, weights, t, rhs, rhs_scale, start=True, stop=True):
-            codes, scales = weights[t // 2]
-            cols = slice(P * (t % 2), P * (t % 2 + 1))
+            per = 4 // len(weights)
+            codes, scales = weights[t // per]
+            cols = slice(P * (t % per), P * (t % per + 1))
             nc.tensor.matmul_mx(
                 out=out,
                 lhsT=codes[:, cols].bitcast(FP8X4),
@@ -136,9 +142,9 @@ def tile_picked_wdime_silu_lo_kernel(
 
         def sum_terms(z_bf, term0, term1):
             nc.vector.tensor_tensor(
-                z_bf.rearrange("p (c i t) -> p c t i", i=4, t=4),
-                term0.rearrange("p t (c i) -> p c t i", i=4),
-                term1.rearrange("p t (c i) -> p c t i", i=4),
+                z_bf.rearrange("p (c i t) -> p c t i", i=2, t=4),
+                term0.rearrange("p t (c i) -> p c t i", i=2),
+                term1.rearrange("p t (c i) -> p c t i", i=2),
                 ADD,
             )
             return z_bf
@@ -151,7 +157,7 @@ def tile_picked_wdime_silu_lo_kernel(
                 s = t % per_bank
                 product(accs[t // per_bank][:, width * s : width * (s + 1)], w2_q, t, codes.bitcast(FP8X4), scales)
 
-        def finish_y(accs, v0, width):
+        def finish_y(accs, v0, width, queue=nc.sync):
             y = f32("y%d" % v0, 4, width)
             per_bank = 4 // len(accs)
             for b, acc in enumerate(accs):
@@ -160,7 +166,7 @@ def tile_picked_wdime_silu_lo_kernel(
                     in_=acc[:, 0 : per_bank * width],
                     func=SILU,
                 )
-            nc.sync.dma_start(out=y_rows[:, :, v0 : v0 + width], in_=y)
+            queue.dma_start(out=y_rows[:, :, v0 : v0 + width], in_=y)
             return y
 
         def silu_woven(woven, acc):
@@ -175,6 +181,8 @@ def tile_picked_wdime_silu_lo_kernel(
         def hand_on(v0, woven_y):
             cols = slice(v0, v0 + woven_y.shape[1] // 4)
             nc.vector.quantize_mx(out=words[:, cols].bitcast(FP8X4), scales=out_scales[:, cols], in_=woven_y)
+
+        def store_words(cols):
             nc.sync.dma_start(out=word_rows[:, cols], in_=words[:, cols].bitcast(I32))
 
         def store_scales():
@@ -189,13 +197,13 @@ def tile_picked_wdime_silu_lo_kernel(
         a00 = load(f32("a_raw00", 4, 256), a_cols(0, 0, 256))
         w1_raw = [load(f32("w1_raw0", 4, 512), w1[0:512, :])]
         load_x()
-        w1_raw.append(load(f32("w1_raw1", 4, 512), w1[512:1024, :]))
+        w1_late = [load(f32("w1_late%d" % c, 4, 256), w1[512:1024, 256 * c : 256 * (c + 1)]) for c in range(2)]
         a10 = load(f32("a_raw10", 4, 256), a_cols(1, 0, 256))
         nc.sync.dma_start(lists[0][:], pos1)
         nc.sync.dma_start(lists[1][:], pos2)
-        a01 = load(f32("a_raw01", 4, 256), a_cols(0, 256, 256))
-        shared = f32("shared", 7, 256)
-        a11 = load(shared[:, 3:7, :], a_cols(1, 256, 256))
+        shared = f32("shared", 13, 256)
+        a01 = load(shared[:, 5:9, :], a_cols(0, 256, 256))
+        a11 = load(shared[:, 9:13, :], a_cols(1, 256, 256))
         w2_raw = load(f32("w2_raw", 4, 512), w2)
 
         woven = [round_weights(bf("w3_bf%d" % u, 1024), w3_raw, u, "vs"[u]) for u in range(2)]
@@ -204,44 +212,50 @@ def tile_picked_wdime_silu_lo_kernel(
         f00 = filters("f00a", bank(4), w3_q, q00, [0, 1], "s")
         f00 = f00 + filters("f00b", bank(5), w3_q, q00, [2, 3], "s")
         acc_h = [bank(t) for t in range(4)]
-        for z in range(2):
-            woven = [round_weights(bf("w1_bf%d%d" % (z, u), 1024), w1_raw[z], u, "vs"[u]) for u in range(2)]
-            w1_q = [quantize("w1_%d%d" % (z, u), woven[u]) for u in range(2)]
-            layer1(acc_h, w1_q, z, range(4))
+        woven = [round_weights(bf("w1_bf0%d" % u, 1024), w1_raw[0], u, "v") for u in range(2)]
+        w1_q = [quantize("w1_0%d" % u, woven[u]) for u in range(2)]
+        layer1(acc_h, w1_q, 0, range(4))
+        woven = [bf("w1_bf1%d" % u, 1024) for u in range(2)]
+        for c in range(2):
+            for u in range(2):
+                round_half(woven[u], w1_late[c], u, c, "vs"[u])
+        w1_q = [quantize("w1_1%d" % t, woven[t // 2][:, 512 * (t % 2) : 512 * (t % 2 + 1)]) for t in range(4)]
+        layer1(acc_h, w1_q, 1, range(4))
         for t in range(4):
             finish_h(acc_h, t)
         q10 = quantize("a10", round_columns(bf("a_bf10", 1024), a10, "v"))
         f10 = filters("f10a", bank(6), w3_q, q10, [0, 1], "s")
         f10 = f10 + filters("f10b", bank(7), w3_q, q10, [2, 3], "s")
         t00 = gathers(0, 0, f32("term00", 4, 256), f00)
-        q01 = quantize("a01", round_columns(bf("a_bf01", 1024), a01, "v"))
+        q01 = quantize("a01", round_columns(bf("a_bf01", 1024), a01, "s"))
         woven_a = round_columns(bf("a_bf11", 1024), a11, "s")
         f01 = filters("f01a", bank(4), w3_q, q01, [0, 1], "s")
         f01 = f01 + filters("f01b", bank(5), w3_q, q01, [2, 3], "s")
         q11 = quantize("a11", woven_a)
-        woven = [round_weights(bf("w2_bf0", 1024), w2_raw, 0, "s")]
         f11 = filters("f11a", bank(6), w3_q, q11, [0, 1], "s")
         f11 = f11 + filters("f11b", bank(7), w3_q, q11, [2, 3], "s")
-        woven.append(round_weights(bf("w2_bf1", 1024), w2_raw, 1, "s"))
+        woven = [round_weights(bf("w2_bf%d" % u, 1024), w2_raw, u, "s") for u in range(2)]
         w2_q = [quantize("w2_%d" % u, woven[u]) for u in range(2)]
-        t10 = gathers(1, 0, shared[:, 0:4, :], f10)
+        t10 = gathers(1, 0, shared[:, 0:13:4, :], f10)
         z0 = quantize("z0", sum_terms(bf("z_bf0", 1024), t00, t10))
         acc0 = [bank(0), bank(1)]
         project(acc0, w2_q, z0)
         y0 = finish_y(acc0, 0, 256)
         t01 = gathers(0, 256, f32("term01", 4, 256), f01)
-        t11 = gathers(1, 256, w2_raw[:, :, 0:128], f11)
-        z1 = quantize("z1", sum_terms(bf("z_bf1", 512), t01[:, :, 0:128], t11))
-        acc1 = [bank(2)]
-        project(acc1, w2_q, z1)
-        y1 = finish_y(acc1, 256, 128)
-        t12 = gathers(1, 384, w2_raw[:, :, 128:256], f11, 128)
-        z2 = quantize("z2", sum_terms(bf("z_bf2", 512), t01[:, :, 128:256], t12))
-        acc2 = [bank(3)]
-        project(acc2, w2_q, z2)
-        woven_y2 = silu_woven(bf("y_bf2", 512), acc2[0])
-        finish_y(acc2, 384, 128)
+        term = gathers(1, 256, w2_raw[:, :, 0:128], f11, 0)
+        z = quantize("z256", sum_terms(bf("z_bf256", 512), t01[:, :, 0:128], term))
+        acc = [bank(4)]
+        project(acc, w2_q, z)
+        y256 = finish_y(acc, 256, 128)
+        term = gathers(1, 384, w2_raw[:, :, 128:256], f11, 128)
+        z = quantize("z384", sum_terms(bf("z_bf384", 512), t01[:, :, 128:256], term))
+        acc = [bank(5)]
+        project(acc, w2_q, z)
+        woven_y1 = silu_woven(bf("y_bf384", 512), acc[0])
+        finish_y(acc, 384, 128, nc.scalar)
         hand_on(0, round_columns(bf("y_bf0", 1024), y0, "s"))
-        hand_on(256, round_columns(bf("y_bf1", 512), y1, "s"))
-        hand_on(384, woven_y2)
+        hand_on(256, round_columns(bf("y_bf256", 512), y256, "v"))
+        store_words(slice(0, 384))
+        hand_on(384, woven_y1)
+        store_words(slice(384, 512))
         store_scales()

@@ -121,12 +121,11 @@ def tile_picked_wdime_silu_lo_kernel(
         def finish_h(acc, t):
             nc.scalar.activation(out=h[t][:], in_=acc[t], func=SILU)
 
-        def filters(name, acc, w3_q, a_q, ts, engine):
+        def filters(f, acc, w3_q, a_q, ts, engine):
             codes, scales = a_q
             width = codes.shape[1]
             for s, t in enumerate(ts):
                 product(acc[:, width * s : width * (s + 1)], w3_q, t, codes.bitcast(FP8X4), scales)
-            f = f32(name, len(ts), width)
             copy_on(engine, f.rearrange("p s c -> p (s c)"), acc[:, 0 : width * len(ts)])
             return [f[:, s, :] for s in range(len(ts))]
 
@@ -142,9 +141,9 @@ def tile_picked_wdime_silu_lo_kernel(
 
         def sum_terms(z_bf, term0, term1):
             nc.vector.tensor_tensor(
-                z_bf.rearrange("p (c i t) -> p c t i", i=2, t=4),
-                term0.rearrange("p t (c i) -> p c t i", i=2),
-                term1.rearrange("p t (c i) -> p c t i", i=2),
+                z_bf.rearrange("p (c i t) -> p c t i", i=4, t=4),
+                term0.rearrange("p t (c i) -> p c t i", i=4),
+                term1.rearrange("p t (c i) -> p c t i", i=4),
                 ADD,
             )
             return z_bf
@@ -193,69 +192,77 @@ def tile_picked_wdime_silu_lo_kernel(
                     in_=out_scales[32 * q : 32 * q + 4, :].bitcast(I32),
                 )
 
-        w3_raw = load(f32("w3_raw", 4, 512), w3)
-        a00 = load(f32("a_raw00", 4, 256), a_cols(0, 0, 256))
         w1_raw = [load(f32("w1_raw0", 4, 512), w1[0:512, :])]
         load_x()
-        w1_late = [load(f32("w1_late%d" % c, 4, 256), w1[512:1024, 256 * c : 256 * (c + 1)]) for c in range(2)]
+        w1_raw.append(load(f32("w1_raw1", 4, 512), w1[512:1024, :]))
+        a00 = load(f32("a_raw00", 4, 256), a_cols(0, 0, 256))
+        w3_raw = load(f32("w3_raw", 4, 512), w3)
         a10 = load(f32("a_raw10", 4, 256), a_cols(1, 0, 256))
         nc.sync.dma_start(lists[0][:], pos1)
         nc.sync.dma_start(lists[1][:], pos2)
-        shared = f32("shared", 13, 256)
-        a01 = load(shared[:, 5:9, :], a_cols(0, 256, 256))
-        a11 = load(shared[:, 9:13, :], a_cols(1, 256, 256))
+        shared = f32("shared", 7, 256)
+        a01 = load(shared[:, 3:7, :], a_cols(0, 256, 256))
+        a11 = load(f32("a_raw11", 4, 256), a_cols(1, 256, 256))
         w2_raw = load(f32("w2_raw", 4, 512), w2)
 
-        woven = [round_weights(bf("w3_bf%d" % u, 1024), w3_raw, u, "vs"[u]) for u in range(2)]
-        w3_q = [quantize("w3_%d" % u, woven[u]) for u in range(2)]
-        q00 = quantize("a00", round_columns(bf("a_bf00", 1024), a00, "v"))
-        f00 = filters("f00a", bank(4), w3_q, q00, [0, 1], "s")
-        f00 = f00 + filters("f00b", bank(5), w3_q, q00, [2, 3], "s")
         acc_h = [bank(t) for t in range(4)]
-        woven = [round_weights(bf("w1_bf0%d" % u, 1024), w1_raw[0], u, "v") for u in range(2)]
-        w1_q = [quantize("w1_0%d" % u, woven[u]) for u in range(2)]
-        layer1(acc_h, w1_q, 0, range(4))
-        woven = [bf("w1_bf1%d" % u, 1024) for u in range(2)]
-        for c in range(2):
-            for u in range(2):
-                round_half(woven[u], w1_late[c], u, c, "vs"[u])
-        w1_q = [quantize("w1_1%d" % t, woven[t // 2][:, 512 * (t % 2) : 512 * (t % 2 + 1)]) for t in range(4)]
-        layer1(acc_h, w1_q, 1, range(4))
-        for t in range(4):
-            finish_h(acc_h, t)
-        q10 = quantize("a10", round_columns(bf("a_bf10", 1024), a10, "v"))
-        f10 = filters("f10a", bank(6), w3_q, q10, [0, 1], "s")
-        f10 = f10 + filters("f10b", bank(7), w3_q, q10, [2, 3], "s")
+        for z in range(2):
+            woven = [round_weights(bf("w1_bf%d%d" % (z, u), 1024), w1_raw[z], u, "vs"[u]) for u in range(2)]
+            w1_q = [quantize("w1_%d%d" % (z, u), woven[u]) for u in range(2)]
+            layer1(acc_h, w1_q, z, range(4))
+        q00 = quantize("a00", round_columns(bf("a_bf00", 1024), a00, "v"))
+        finish_h(acc_h, 0)
+        finish_h(acc_h, 1)
+        finish_h(acc_h, 2)
+        finish_h(acc_h, 3)
+        woven = [round_weights(bf("w3_bf%d" % u, 1024), w3_raw, u, "vv"[u]) for u in range(2)]
+        w3_q = [quantize("w3_%d" % t, woven[t // 2][:, 512 * (t % 2) : 512 * (t % 2 + 1)]) for t in range(4)]
+        f00a = f32("f00a", 2, 256)
+        f00 = filters(f00a[:, 0:1, :], bank(4), w3_q, q00, [0], "s")
+        f00 = f00 + filters(f00a[:, 1:2, :], bank(5), w3_q, q00, [1], "s")
+        f00b = f32("f00b", 3, 256)
+        f00 = f00 + filters(f00b[:, 1:3, :], bank(6), w3_q, q00, [2, 3], "s")
+        a_bf10 = bf("a_bf10", 1024)
+        round_columns(a_bf10[:, 0:512], a10[:, :, 0:128], "s")
+        round_columns(a_bf10[:, 512:1024], a10[:, :, 128:256], "v")
+        q10 = quantize("a10", a_bf10)
+        f10a = f32("f10a", 3, 256)
+        f10 = filters(f10a[:, 1:3, :], bank(7), w3_q, q10, [0, 1], "s")
+        f10 = f10 + filters(f32("f10b", 2, 256), bank(0), w3_q, q10, [2, 3], "s")
         t00 = gathers(0, 0, f32("term00", 4, 256), f00)
-        q01 = quantize("a01", round_columns(bf("a_bf01", 1024), a01, "s"))
-        woven_a = round_columns(bf("a_bf11", 1024), a11, "s")
-        f01 = filters("f01a", bank(4), w3_q, q01, [0, 1], "s")
-        f01 = f01 + filters("f01b", bank(5), w3_q, q01, [2, 3], "s")
+        t10 = shared[:, 1:5, :]
+        for t in range(2):
+            gather(1, 0, t, t10, f10[t])
+        q01 = quantize("a01", round_columns(f00b[:, 0:2, :].rearrange("p t c -> p (t c)").bitcast(BF16), a01, "s"))
+        woven_a = round_columns(f10a[:, 0:2, :].rearrange("p t c -> p (t c)").bitcast(BF16), a11, "s")
+        f01 = filters(f32("f01a", 2, 256), bank(1), w3_q, q01, [0, 1], "s")
+        f01 = f01 + filters(f32("f01b", 2, 256), bank(2), w3_q, q01, [2, 3], "s")
         q11 = quantize("a11", woven_a)
-        f11 = filters("f11a", bank(6), w3_q, q11, [0, 1], "s")
-        f11 = f11 + filters("f11b", bank(7), w3_q, q11, [2, 3], "s")
+        f11 = filters(f32("f11a", 2, 256), bank(3), w3_q, q11, [0, 1], "s")
+        f11 = f11 + filters(f32("f11b", 2, 256), bank(4), w3_q, q11, [2, 3], "s")
         woven = [round_weights(bf("w2_bf%d" % u, 1024), w2_raw, u, "s") for u in range(2)]
         w2_q = [quantize("w2_%d" % u, woven[u]) for u in range(2)]
-        t10 = gathers(1, 0, shared[:, 0:13:4, :], f10)
-        z0 = quantize("z0", sum_terms(bf("z_bf0", 1024), t00, t10))
-        acc0 = [bank(0), bank(1)]
+        for t in range(2, 4):
+            gather(1, 0, t, t10, f10[t])
+        z_bf0 = a11[:, 0:2, :].rearrange("p j c -> p (j c)").bitcast(BF16)
+        z0 = quantize("z0", sum_terms(z_bf0, t00, t10))
+        acc0 = [bank(5), bank(6)]
         project(acc0, w2_q, z0)
         y0 = finish_y(acc0, 0, 256)
         t01 = gathers(0, 256, f32("term01", 4, 256), f01)
         term = gathers(1, 256, w2_raw[:, :, 0:128], f11, 0)
         z = quantize("z256", sum_terms(bf("z_bf256", 512), t01[:, :, 0:128], term))
-        acc = [bank(4)]
+        acc = [bank(7)]
         project(acc, w2_q, z)
         y256 = finish_y(acc, 256, 128)
         term = gathers(1, 384, w2_raw[:, :, 128:256], f11, 128)
         z = quantize("z384", sum_terms(bf("z_bf384", 512), t01[:, :, 128:256], term))
-        acc = [bank(5)]
+        acc = [bank(0)]
         project(acc, w2_q, z)
-        woven_y1 = silu_woven(bf("y_bf384", 512), acc[0])
-        finish_y(acc, 384, 128, nc.scalar)
+        y384 = finish_y(acc, 384, 128, nc.scalar)
         hand_on(0, round_columns(bf("y_bf0", 1024), y0, "s"))
         hand_on(256, round_columns(bf("y_bf256", 512), y256, "v"))
         store_words(slice(0, 384))
-        hand_on(384, woven_y1)
+        hand_on(384, round_columns(bf("y_bf384", 512), y384, "v"))
         store_words(slice(384, 512))
         store_scales()

@@ -54,6 +54,11 @@ def tile_picked_wdime_silu_lo_kernel(
             dst = dealt.rearrange("p (t m j) -> p m j t", t=2, j=4)[:, 64 * half : 64 * (half + 1), :, :]
             copy_on(engine, dst, src)
 
+        def round_hidden(dealt, raw, t0, count, engine):
+            src = raw.rearrange("p j (a t b) -> p a t j b", t=4, b=4)[:, :, t0 : t0 + count, :, :]
+            copy_on(engine, dealt.rearrange("p (t a b j) -> p a t j b", t=count, b=4, j=4), src)
+            return dealt
+
         def round_columns(woven, planes, engine):
             copy_on(
                 engine,
@@ -203,11 +208,16 @@ def tile_picked_wdime_silu_lo_kernel(
         shared = f32("shared", 7, 256)
         a01 = load(shared[:, 3:7, :], a_cols(0, 256, 256))
         a11 = load(f32("a_raw11", 4, 256), a_cols(1, 256, 256))
-        w2_raw = load(f32("w2_raw", 4, 512), w2)
+        late = f32("late", 5, 512)
+        w2_raw = late[:, 1:5, :]
+        for b in range(4):
+            nc.sync.dma_start(
+                out=w2_raw[b:P:4, :, :], in_=w2.rearrange("(a t b) n -> b a t n", t=4, b=4)[b]
+            )
 
         acc_h = [bank(t) for t in range(4)]
         for z in range(2):
-            woven = [round_weights(bf("w1_bf%d%d" % (z, u), 1024), w1_raw[z], u, "vs"[u]) for u in range(2)]
+            woven = [round_hidden(bf("u1_bf%d%d" % (z, u), 1024), w1_raw[z], 2 * u, 2, "vs"[u]) for u in range(2)]
             w1_q = [quantize("w1_%d%d" % (z, u), woven[u]) for u in range(2)]
             layer1(acc_h, w1_q, z, range(4))
         q00 = quantize("a00", round_columns(bf("a_bf00", 1024), a00, "v"))
@@ -215,8 +225,7 @@ def tile_picked_wdime_silu_lo_kernel(
         finish_h(acc_h, 1)
         finish_h(acc_h, 2)
         finish_h(acc_h, 3)
-        woven = [round_weights(bf("w3_bf%d" % u, 1024), w3_raw, u, "vv"[u]) for u in range(2)]
-        w3_q = [quantize("w3_%d" % t, woven[t // 2][:, 512 * (t % 2) : 512 * (t % 2 + 1)]) for t in range(4)]
+        w3_q = [quantize("w3_%d" % t, round_hidden(bf("u3_bf%d" % t, 512), w3_raw, t, 1, "v")) for t in range(4)]
         f00a = f32("f00a", 2, 256)
         f00 = filters(f00a[:, 0:1, :], bank(4), w3_q, q00, [0], "s")
         f00 = f00 + filters(f00a[:, 1:2, :], bank(5), w3_q, q00, [1], "s")
@@ -250,12 +259,12 @@ def tile_picked_wdime_silu_lo_kernel(
         project(acc0, w2_q, z0)
         y0 = finish_y(acc0, 0, 256)
         t01 = gathers(0, 256, f32("term01", 4, 256), f01)
-        term = gathers(1, 256, w2_raw[:, :, 0:128], f11, 0)
+        term = gathers(1, 256, late[:, 0:2, :].rearrange("p a (b c) -> p (a b) c", b=2)[:, :, 0:128], f11, 0)
         z = quantize("z256", sum_terms(bf("z_bf256", 512), t01[:, :, 0:128], term))
         acc = [bank(7)]
         project(acc, w2_q, z)
         y256 = finish_y(acc, 256, 128)
-        term = gathers(1, 384, w2_raw[:, :, 128:256], f11, 128)
+        term = gathers(1, 384, w2_raw[:, :, 384:512], f11, 128)
         z = quantize("z384", sum_terms(bf("z_bf384", 512), t01[:, :, 128:256], term))
         acc = [bank(0)]
         project(acc, w2_q, z)

@@ -200,10 +200,10 @@ def tile_picked_wdime_silu_lo_kernel(
         w1_raw = [load(f32("w1_raw0", 4, 512), w1[0:512, :])]
         load_x()
         w1_raw.append(load(f32("w1_raw1", 4, 512), w1[512:1024, :]))
+        nc.sync.dma_start(lists[0][:], pos1)
         a00 = load(f32("a_raw00", 4, 256), a_cols(0, 0, 256))
         w3_raw = load(f32("w3_raw", 4, 512), w3)
         a10 = load(f32("a_raw10", 4, 256), a_cols(1, 0, 256))
-        nc.sync.dma_start(lists[0][:], pos1)
         nc.sync.dma_start(lists[1][:], pos2)
         shared = f32("shared", 7, 256)
         a01 = load(shared[:, 3:7, :], a_cols(0, 256, 256))
@@ -216,19 +216,26 @@ def tile_picked_wdime_silu_lo_kernel(
             )
 
         acc_h = [bank(t) for t in range(4)]
-        for z in range(2):
-            woven = [round_hidden(bf("u1_bf%d%d" % (z, u), 1024), w1_raw[z], 2 * u, 2, "vs"[u]) for u in range(2)]
-            w1_q = [quantize("w1_%d%d" % (z, u), woven[u]) for u in range(2)]
-            layer1(acc_h, w1_q, z, range(4))
+        woven = [round_hidden(bf("u1_bf0%d" % u, 1024), w1_raw[0], 2 * u, 2, "vs"[u]) for u in range(2)]
+        w1_q = [quantize("w1_0%d" % u, woven[u]) for u in range(2)]
+        layer1(acc_h, w1_q, 0, range(4))
+        w1_q = [quantize("w1_1%d" % t, round_hidden(bf("u1_bf1%d" % t, 512), w1_raw[1], t, 1, "vvvv"[t])) for t in range(4)]
+        layer1(acc_h, w1_q, 1, range(4))
         q00 = quantize("a00", round_columns(bf("a_bf00", 1024), a00, "v"))
         finish_h(acc_h, 0)
         finish_h(acc_h, 1)
+        early = f32("early", 1, 256)
+        for t in range(1):
+            nc.vector.tensor_copy(early[:, t, :], h[t][:].indirect(lists[0][:, 0:16]))
         finish_h(acc_h, 2)
         finish_h(acc_h, 3)
-        w3_q = [quantize("w3_%d" % t, round_hidden(bf("u3_bf%d" % t, 512), w3_raw, t, 1, "v")) for t in range(4)]
-        f00a = f32("f00a", 2, 256)
-        f00 = filters(f00a[:, 0:1, :], bank(4), w3_q, q00, [0], "s")
-        f00 = f00 + filters(f00a[:, 1:2, :], bank(5), w3_q, q00, [1], "s")
+        w3_q = [quantize("w3_%d" % t, round_hidden(bf("u3_bf%d" % t, 512), w3_raw, t, 1, "vvvs"[t])) for t in range(4)]
+        t00 = f32("term00", 4, 256)
+        for t in range(1):
+            acc = bank(4 + t)[:, 0:256]
+            product(acc, w3_q, t, q00[0].bitcast(FP8X4), q00[1])
+            nc.vector.tensor_tensor(t00[:, t, :], early[:, t, :], acc, MULT)
+        f00 = [None] + filters(f32("f00a", 1, 256), bank(5), w3_q, q00, [1], "s")
         f00b = f32("f00b", 3, 256)
         f00 = f00 + filters(f00b[:, 1:3, :], bank(6), w3_q, q00, [2, 3], "s")
         a_bf10 = bf("a_bf10", 1024)
@@ -238,8 +245,9 @@ def tile_picked_wdime_silu_lo_kernel(
         f10a = f32("f10a", 3, 256)
         f10 = filters(f10a[:, 1:3, :], bank(7), w3_q, q10, [0, 1], "s")
         f10 = f10 + filters(f32("f10b", 2, 256), bank(0), w3_q, q10, [2, 3], "s")
-        t00 = gathers(0, 0, f32("term00", 4, 256), f00)
-        t10 = shared[:, 1:5, :]
+        for t in range(1, 4):
+            gather(0, 0, t, t00, f00[t])
+        t10 = shared[:, 0:4, :]
         for t in range(2):
             gather(1, 0, t, t10, f10[t])
         q01 = quantize("a01", round_columns(f00b[:, 0:2, :].rearrange("p t c -> p (t c)").bitcast(BF16), a01, "s"))
@@ -259,14 +267,14 @@ def tile_picked_wdime_silu_lo_kernel(
         project(acc0, w2_q, z0)
         y0 = finish_y(acc0, 0, 256)
         t01 = gathers(0, 256, f32("term01", 4, 256), f01)
-        term = gathers(1, 256, late[:, 0:2, :].rearrange("p a (b c) -> p (a b) c", b=2)[:, :, 0:128], f11, 0)
+        term = gathers(1, 256, late[:, 0:2, :].rearrange("p a (b c) -> p (a b) c", b=4)[:, 1:5, :], f11, 0)
         z = quantize("z256", sum_terms(bf("z_bf256", 512), t01[:, :, 0:128], term))
         acc = [bank(7)]
         project(acc, w2_q, z)
         y256 = finish_y(acc, 256, 128)
         term = gathers(1, 384, w2_raw[:, :, 384:512], f11, 128)
         z = quantize("z384", sum_terms(bf("z_bf384", 512), t01[:, :, 128:256], term))
-        acc = [bank(0)]
+        acc = [bank(0), bank(1)]
         project(acc, w2_q, z)
         y384 = finish_y(acc, 384, 128, nc.scalar)
         hand_on(0, round_columns(bf("y_bf0", 1024), y0, "s"))

from contextlib import ExitStack

import concourse.mybir as mybir

K, T, H, J = 1024, 512, 512, 512
FLOPS = 2 * (K * H * T + J * H * 2 * T + H * H * T)

F32 = mybir.dt.float32
BF16 = mybir.dt.bfloat16
I32 = mybir.dt.int32
U32 = mybir.dt.uint32
U16 = mybir.dt.uint16
U8 = mybir.dt.uint8
FP8X4 = mybir.dt.float8_e4m3fn_x4
FP4X4 = mybir.dt.float4_e2m1fn_x4
SILU = mybir.ActivationFunctionType.Silu
MULT = mybir.AluOpType.mult
ADD = mybir.AluOpType.add

P = 128


def tile_picked_wdime_silu_lo_kernel(
    tc, x_words, x_scales, aT, w1, w3, w2, pos1, pos2, out_0, out_1, out_2
):
    nc = tc.nc
    with ExitStack() as ctx:
        sb = ctx.enter_context(tc.tile_pool(name="sb", bufs=1))
        ps = ctx.enter_context(tc.psum_pool(name="ps", bufs=1))

        def tile(name, shape, dtype):
            return sb.tile(shape, dtype, name=name, align_bytes=64)[:]

        def bank(b):
            return ps.tile([P, 512], F32, name="bank%d" % b)[:]

        def copy_on(engine, out, in_):
            if engine == "v":
                nc.vector.tensor_copy(out=out, in_=in_)
            else:
                nc.scalar.copy(out=out, in_=in_)

        def load(raw, rows):
            nc.sync.dma_start(out=raw, in_=rows.rearrange("(p j) w -> p j w", j=4))
            return raw

        def round_weights(dealt, raw, u, engine):
            src = raw.rearrange("p j (m t) -> p m j t", t=4)[:, :, :, 2 * u : 2 * u + 2]
            copy_on(engine, dealt.rearrange("p (t m j) -> p m j t", t=2, j=4), src)
            return dealt

        def round_half(dealt, raw, u, half, engine):
            src = raw.rearrange("p j (m t) -> p m j t", t=4)[:, :, :, 2 * u : 2 * u + 2]
            dst = dealt.rearrange("p (t m j) -> p m j t", t=2, j=4)[:, 64 * half : 64 * (half + 1), :, :]
            copy_on(engine, dst, src)

        def round_hidden(dealt, raw, t0, count, engine):
            src = raw.rearrange("p j (a t b) -> p a t j b", t=4, b=4)[:, :, t0 : t0 + count, :, :]
            copy_on(engine, dealt.rearrange("p (t a b j) -> p a t j b", t=count, b=4, j=4), src)
            return dealt

        def round_columns(woven, planes, engine):
            copy_on(
                engine,
                woven.rearrange("p (c i j) -> p c j i", i=4, j=4),
                planes.rearrange("p j (c i) -> p c j i", i=4),
            )
            return woven

        def quantize(name, woven):
            width = woven.shape[1] // 4
            codes = tile(name + "_codes", [P, width], U32)
            scales = tile(name + "_scales", [P, width], U8)
            nc.vector.quantize_mx(out=codes.bitcast(FP8X4), scales=scales, in_=woven)
            return codes, scales

        def product(out, weights, t, rhs, rhs_scale, start=True, stop=True):
            per = 4 // len(weights)
            codes, scales = weights[t // per]
            cols = slice(P * (t % per), P * (t % per + 1))
            nc.tensor.matmul_mx(
                out=out,
                lhsT=codes[:, cols].bitcast(FP8X4),
                lhsT_scale=scales[:, cols],
                rhs=rhs,
                rhs_scale=rhs_scale,
                start=start,
                stop=stop,
            )

        def bf(name, n):
            return tile(name, [P, n], BF16)

        def f32(name, a, b):
            return tile(name, [P, a, b], F32)

        lists = [sb.tile([P, T // 16], U16, name="list0"), sb.tile([P, T // 16], U16, name="list1")]
        h = [sb.tile([P, T], F32, name="h%d" % t) for t in range(4)]
        xs = tile("xs", [P, 2, T], U8)
        xw = tile("xw", [P, 2, 2 * T], U8)
        words = tile("words", [P, T], U32)
        out_scales = tile("out_scales", [P, T], U8)
        y_rows = out_0.rearrange("(p t) v -> p t v", t=4)
        word_rows = out_1[0].rearrange("p c r -> p (c r)").bitcast(I32)

        warm = tile("warm", [P, 1], F32)
        warmed = tile("warmed", [P, 1], F32)
        nc.vector.memset(warm, 0.0)
        nc.scalar.activation(out=warmed, in_=warm, func=SILU)

        def load_x():
            nc.sync.dma_start(out=xw.bitcast(I32), in_=x_words.rearrange("z p c -> p z c").bitcast(I32))
            for q in range(4):
                nc.sync.dma_start(
                    out=xs[32 * q : 32 * q + 4, :, :].bitcast(I32),
                    in_=x_scales[:, 4 * q : 4 * q + 4, :].rearrange("z r c -> r z c").bitcast(I32),
                )

        def a_cols(d, v0, width):
            return aT[:, T * d + v0 : T * d + v0 + width]

        def layer1(acc, w1_q, z, ts):
            for t in ts:
                product(acc[t], w1_q, t, xw[:, z, :].bitcast(FP4X4), xs[:, z, :], z == 0, z == 1)

        def finish_h(acc, t):
            nc.scalar.activation(out=h[t][:], in_=acc[t], func=SILU)

        def filters(f, acc, w3_q, a_q, ts, engine):
            codes, scales = a_q
            width = codes.shape[1]
            for s, t in enumerate(ts):
                product(acc[:, width * s : width * (s + 1)], w3_q, t, codes.bitcast(FP8X4), scales)
            copy_on(engine, f.rearrange("p s c -> p (s c)"), acc[:, 0 : width * len(ts)])
            return [f[:, s, :] for s in range(len(ts))]

        def gather(d, v0, t, term, f):
            width = term.shape[2]
            offsets = lists[d][:, v0 // 16 : (v0 + width) // 16]
            nc.vector.tensor_tensor(term[:, t, :], h[t][:].indirect(offsets), f, MULT)

        def gathers(d, v0, term, fs, lo=0):
            for t in range(4):
                gather(d, v0, t, term, fs[t][:, lo : lo + term.shape[2]])
            return term

        def sum_terms(z_bf, term0, term1):
            nc.vector.tensor_tensor(
                z_bf.rearrange("p (c i t) -> p c t i", i=4, t=4),
                term0.rearrange("p t (c i) -> p c t i", i=4),
                term1.rearrange("p t (c i) -> p c t i", i=4),
                ADD,
            )
            return z_bf

        def project(accs, w2_q, z_q):
            codes, scales = z_q
            width = codes.shape[1]
            per_bank = 4 // len(accs)
            for t in range(4):
                s = t % per_bank
                product(accs[t // per_bank][:, width * s : width * (s + 1)], w2_q, t, codes.bitcast(FP8X4), scales)

        def finish_y(accs, v0, width, queue=nc.sync):
            y = f32("y%d" % v0, 4, width)
            per_bank = 4 // len(accs)
            for b, acc in enumerate(accs):
                nc.scalar.activation(
                    out=y[:, per_bank * b : per_bank * (b + 1), :].rearrange("p t c -> p (t c)"),
                    in_=acc[:, 0 : per_bank * width],
                    func=SILU,
                )
            queue.dma_start(out=y_rows[:, :, v0 : v0 + width], in_=y)
            return y

        def silu_woven(woven, acc):
            width = woven.shape[1] // 4
            nc.scalar.activation(
                out=woven.rearrange("p (c t) -> p c t", t=4),
                in_=acc[:, 0 : 4 * width].rearrange("p (t c) -> p c t", t=4),
                func=SILU,
            )
            return woven

        def hand_on(v0, woven_y):
            cols = slice(v0, v0 + woven_y.shape[1] // 4)
            nc.vector.quantize_mx(out=words[:, cols].bitcast(FP8X4), scales=out_scales[:, cols], in_=woven_y)

        def store_words(cols):
            nc.sync.dma_start(out=word_rows[:, cols], in_=words[:, cols].bitcast(I32))

        def store_scales():
            for q in range(4):
                queue = nc.sync if q % 2 else nc.scalar
                queue.dma_start(
                    out=out_2[0, 4 * q : 4 * q + 4, :].bitcast(I32),
                    in_=out_scales[32 * q : 32 * q + 4, :].bitcast(I32),
                )

        w1_raw = [load(f32("w1_raw0", 4, 512), w1[0:512, :])]
        load_x()
        w1_raw.append(load(f32("w1_raw1", 4, 512), w1[512:1024, :]))
        nc.sync.dma_start(lists[0][:], pos1)
        a00 = load(f32("a_raw00", 4, 256), a_cols(0, 0, 256))
        w3_raw = load(f32("w3_raw", 4, 512), w3)
        a10 = load(f32("a_raw10", 4, 256), a_cols(1, 0, 256))
        nc.sync.dma_start(lists[1][:], pos2)
        shared = f32("shared", 7, 256)
        a01 = load(shared[:, 3:7, :], a_cols(0, 256, 256))
        a11 = load(f32("a_raw11", 4, 256), a_cols(1, 256, 256))
        late = f32("late", 5, 512)
        w2_raw = late[:, 1:5, :]
        for b in range(4):
            nc.sync.dma_start(
                out=w2_raw[b:P:4, :, :], in_=w2.rearrange("(a t b) n -> b a t n", t=4, b=4)[b]
            )

        acc_h = [bank(t) for t in range(4)]
        woven = [round_hidden(bf("u1_bf0%d" % u, 1024), w1_raw[0], 2 * u, 2, "vs"[u]) for u in range(2)]
        w1_q = [quantize("w1_0%d" % u, woven[u]) for u in range(2)]
        layer1(acc_h, w1_q, 0, range(4))
        w1_q = [quantize("w1_1%d" % t, round_hidden(bf("u1_bf1%d" % t, 512), w1_raw[1], t, 1, "vvvv"[t])) for t in range(4)]
        layer1(acc_h, w1_q, 1, range(4))
        q00 = quantize("a00", round_columns(bf("a_bf00", 1024), a00, "v"))
        finish_h(acc_h, 0)
        finish_h(acc_h, 1)
        early = f32("early", 1, 256)
        for t in range(1):
            nc.vector.tensor_copy(early[:, t, :], h[t][:].indirect(lists[0][:, 0:16]))
        finish_h(acc_h, 2)
        finish_h(acc_h, 3)
        w3_q = [quantize("w3_%d" % t, round_hidden(bf("u3_bf%d" % t, 512), w3_raw, t, 1, "vvvs"[t])) for t in range(4)]
        t00 = f32("term00", 4, 256)
        for t in range(1):
            acc = bank(4 + t)[:, 0:256]
            product(acc, w3_q, t, q00[0].bitcast(FP8X4), q00[1])
            nc.vector.tensor_tensor(t00[:, t, :], early[:, t, :], acc, MULT)
        f00 = [None] + filters(f32("f00a", 1, 256), bank(5), w3_q, q00, [1], "s")
        f00b = f32("f00b", 3, 256)
        f00 = f00 + filters(f00b[:, 1:3, :], bank(6), w3_q, q00, [2, 3], "s")
        a_bf10 = bf("a_bf10", 1024)
        round_columns(a_bf10[:, 0:512], a10[:, :, 0:128], "s")
        round_columns(a_bf10[:, 512:1024], a10[:, :, 128:256], "v")
        q10 = quantize("a10", a_bf10)
        f10a = f32("f10a", 3, 256)
        f10 = filters(f10a[:, 1:3, :], bank(7), w3_q, q10, [0, 1], "s")
        f10 = f10 + filters(f32("f10b", 2, 256), bank(0), w3_q, q10, [2, 3], "s")
        for t in range(1, 4):
            gather(0, 0, t, t00, f00[t])
        t10 = shared[:, 0:4, :]
        for t in range(2):
            gather(1, 0, t, t10, f10[t])
        q01 = quantize("a01", round_columns(f00b[:, 0:2, :].rearrange("p t c -> p (t c)").bitcast(BF16), a01, "s"))
        woven_a = round_columns(f10a[:, 0:2, :].rearrange("p t c -> p (t c)").bitcast(BF16), a11, "s")
        f01 = filters(f32("f01a", 2, 256), bank(1), w3_q, q01, [0, 1], "s")
        f01 = f01 + filters(f32("f01b", 2, 256), bank(2), w3_q, q01, [2, 3], "s")
        q11 = quantize("a11", woven_a)
        f11 = filters(f32("f11a", 2, 256), bank(3), w3_q, q11, [0, 1], "s")
        f11 = f11 + filters(f32("f11b", 2, 256), bank(4), w3_q, q11, [2, 3], "s")
        woven = [round_weights(bf("w2_bf%d" % u, 1024), w2_raw, u, "s") for u in range(2)]
        w2_q = [quantize("w2_%d" % u, woven[u]) for u in range(2)]
        for t in range(2, 4):
            gather(1, 0, t, t10, f10[t])
        z_bf0 = a11[:, 0:2, :].rearrange("p j c -> p (j c)").bitcast(BF16)
        z0 = quantize("z0", sum_terms(z_bf0, t00, t10))
        acc0 = [bank(5), bank(6)]
        project(acc0, w2_q, z0)
        y0 = finish_y(acc0, 0, 256)
        t01 = gathers(0, 256, f32("term01", 4, 256), f01)
        term = gathers(1, 256, late[:, 0:2, :].rearrange("p a (b c) -> p (a b) c", b=4)[:, 1:5, :], f11, 0)
        z = quantize("z256", sum_terms(bf("z_bf256", 512), t01[:, :, 0:128], term))
        acc = [bank(7)]
        project(acc, w2_q, z)
        y256 = finish_y(acc, 256, 128)
        term = gathers(1, 384, w2_raw[:, :, 384:512], f11, 128)
        z = quantize("z384", sum_terms(bf("z_bf384", 512), t01[:, :, 128:256], term))
        acc = [bank(0), bank(1)]
        project(acc, w2_q, z)
        y384 = finish_y(acc, 384, 128, nc.scalar)
        hand_on(0, round_columns(bf("y_bf0", 1024), y0, "s"))
        hand_on(256, round_columns(bf("y_bf256", 512), y256, "v"))
        store_words(slice(0, 384))
        hand_on(384, round_columns(bf("y_bf384", 512), y384, "v"))
        store_words(slice(384, 512))
        store_scales()
